import numpy as np
import ml_dtypes


def mxq(x, axis, fmt="e4m3"):
    dtype, down = {"e4m3": (ml_dtypes.float8_e4m3fn, 7), "e5m2": (ml_dtypes.float8_e5m2, 14)}[fmt]
    v = np.moveaxis(np.asarray(x, np.float32).astype(ml_dtypes.bfloat16).astype(np.float64), axis, -1)
    blocks = v.reshape(v.shape[:-1] + (-1, 32))
    amax = np.abs(blocks).max(-1, keepdims=True)
    byte = np.maximum(np.where(amax > 0, np.frexp(amax)[1] - 1 + 127, 0) - down, 1)
    scale = np.exp2(byte - 127.0)
    codes = (blocks / scale).astype(np.float32).astype(dtype).astype(np.float64)
    return np.moveaxis((codes * scale).reshape(v.shape), -1, axis)


WIDE = False


def mx_kscale(k):
    if not WIDE:
        return np.ones(k)
    levels = np.array([10, -10, 5, -5, 0])
    if k % 512:
        return np.exp2(np.random.permutation(np.resize(levels, k // 32))).repeat(32)
    a = np.empty((k // 512, 16))
    for p in range(k // 512):
        a[p, :8] = np.random.permutation(np.resize(levels, 8))
        for g in range(8):
            far = levels[np.abs(levels - a[p, g]) >= 10]
            a[p, g + 8] = far[np.random.randint(len(far))]
    return np.exp2(a.ravel()).repeat(32)


def f64(x):
    return np.asarray(x).astype(np.float64)


def striped(idx):
    return np.tile(idx.reshape(-1, 16).T, (8, 1)).astype(np.uint16)


def unstriped(offs):
    return offs[:16].T.reshape(-1).astype(np.int64)


E2M1 = np.array([0.0, 0.5, 1.0, 1.5, 2.0, 3.0, 4.0, 6.0, -0.0, -0.5, -1.0, -1.5, -2.0, -3.0, -4.0, -6.0])


def pack_weight(w, fmt):
    k, n = w.shape
    w = f64(np.asarray(w, np.float32).astype(ml_dtypes.bfloat16)).reshape(k // 32, 32, n)
    amax = np.abs(w).max(1)
    if fmt == "e4m3":
        byte = np.frexp(amax)[1] - 1 + 127 - 7
    else:
        mant, ex = np.frexp(amax / 6.0)
        byte = np.where(mant > 0.5, ex, ex - 1) + 127
    byte = np.clip(np.where(amax > 0, byte, 1), 1, 254)
    scaled = (w * np.exp2(127.0 - byte)[:, None, :]).reshape(k, n).astype(np.float32)
    by_word = np.ascontiguousarray(scaled.reshape(k // 512, 128, 4, n).transpose(0, 1, 3, 2))
    if fmt == "e4m3":
        words = by_word.astype(ml_dtypes.float8_e4m3fn).view(np.uint8)
    else:
        c = by_word.astype(ml_dtypes.float4_e2m1fn).view(np.uint8) & 0xF
        words = (c[..., 0::2] | (c[..., 1::2] << 4)).reshape(k // 512, 128, 2 * n)
    return np.ascontiguousarray(words), np.ascontiguousarray(byte.astype(np.uint8).reshape(k // 512, 16, n))


def unpack_weight(words, scales, fmt):
    g, _, n = scales.shape
    words = np.ascontiguousarray(words).reshape(g, 128, n, -1)
    if fmt == "e4m3":
        vals = words.view(ml_dtypes.float8_e4m3fn).astype(np.float64)
    else:
        nib = np.empty((g, 128, n, 4), np.uint8)
        nib[..., 0::2] = words & 0xF
        nib[..., 1::2] = words >> 4
        vals = E2M1[nib]
    vals = vals * np.repeat(np.exp2(scales.astype(np.float64) - 127.0), 8, axis=1)[..., None]
    return vals.transpose(0, 1, 3, 2).reshape(g * 512, n)


def gelu(v):
    return 0.5 * v * (1.0 + np.tanh(np.sqrt(2.0 / np.pi) * (v + 0.044715 * v**3)))


K, T, E, N = 1536, 1536, 8, 128
COUNTS = (128, 128, 512, 128, 640, 384, 640, 512)
STARTS = np.cumsum((0,) + COUNTS)


def by_expert(wq, xq):
    return np.concatenate([wq[e].T @ xq[:, STARTS[e]:STARTS[e + 1]] for e in range(E)], axis=1)


def setup_inputs():
    n = np.random.standard_normal
    s = mx_kscale(K)[:, None]
    both = np.repeat(np.arange(E), COUNTS)
    pair = np.stack([both[:T], both[T:]])[:, np.random.permutation(T)]
    pair = np.where(np.random.rand(T) < 0.5, pair, pair[::-1])
    order = np.argsort(pair.reshape(-1), kind="stable")
    slot_token = order % T; pos = np.empty(2 * T, np.int64); pos[order] = np.arange(2 * T); pos = pos.reshape(2, T)
    g = np.random.uniform(0.2, 0.8, T)
    w = [pack_weight(m, "e2m1") for m in n((E, K, N)) / np.sqrt(K) / s[None]]
    return {
        "xT": (n((K, T)) * s).astype(np.float32),
        "w_words": np.stack([m[0] for m in w]),
        "w_scales": np.stack([m[1] for m in w]),
        "b": (0.3 * n((N, E))).astype(np.float32),
        "gate": np.stack([np.tile(g, (N, 1)), np.tile(1.0 - g, (N, 1))]).astype(np.float32),
        "offs": striped(slot_token),
        "pos1": striped(pos[0]),
        "pos2": striped(pos[1]),
    }


def reference(xT, w_words, w_scales, b, gate, offs, pos1, pos2):
    idx = unstriped(offs)
    w = np.stack([unpack_weight(w_words[e], w_scales[e], "e2m1") for e in range(E)])
    xq = mxq(f64(xT)[:, idx], 0, "e4m3")
    y = by_expert(w, xq)
    y = gelu(y + np.repeat(f64(b), COUNTS, axis=1))
    return f64(gate[0]) * y[:, unstriped(pos1)] + f64(gate[1]) * y[:, unstriped(pos2)]

@@ -1,0 +1,219 @@
+from contextlib import ExitStack
+
+import concourse.mybir as mybir
+
+F32 = mybir.dt.float32
+BF16 = mybir.dt.bfloat16
+I32 = mybir.dt.int32
+U32 = mybir.dt.uint32
+U16 = mybir.dt.uint16
+U8 = mybir.dt.uint8
+FP8X4 = mybir.dt.float8_e4m3fn_x4
+FP4X4 = mybir.dt.float4_e2m1fn_x4
+GELU = mybir.ActivationFunctionType.Gelu_apprx_tanh
+MULT = mybir.AluOpType.mult
+
+P = 128
+PACK = 4
+K = 1536
+T = 1536
+PASSES = 3
+E = 8
+N = 128
+S = 3072
+COUNTS = (128, 128, 512, 128, 640, 384, 640, 512)
+FLOPS = 2 * S * K * N
+
+
+def tile_moe_rag_lin_gelu_kernel(tc, xT, w_words, w_scales, b, gate, offs, pos1, pos2, out):
+    nc = tc.nc
+    with ExitStack() as ctx:
+        lists = ctx.enter_context(tc.tile_pool(name="lists", bufs=1))
+        keep = ctx.enter_context(tc.tile_pool(name="keep", bufs=1))
+        psum = ctx.enter_context(tc.psum_pool(name="psum", bufs=1))
+
+        offs_t = lists.tile([P, S // 16], U16, name="offs_t")
+        pos1_t = lists.tile([P, T // 16], U16, name="pos1_t")
+        pos2_t = lists.tile([P, T // 16], U16, name="pos2_t")
+
+        chunks = (
+            ((0, 512), (512, 512), (1024, 256), (1280, 256)),
+            ((0, 512), (512, 512), (1024, 256), (1280, 256)),
+            ((0, 512), (512, 512), (1024, 512)),
+        )
+        vector_copies = {(0, 0), (0, 2), (0, 3)}
+
+        codes = [keep.tile([P, T], U32, name=f"codes{a}", align_bytes=64) for a in range(PASSES)]
+        bytes_all = keep.tile([P, T], U8, name="bytes_all", align_bytes=64)
+        gw = [keep.tile([P, S], U32, name=f"gw{a}", align_bytes=64) for a in range(PASSES)]
+        gb = keep.tile([P, S], U8, name="gb", align_bytes=64)
+        plane1 = keep.tile([P, S], U8, name="plane1", align_bytes=64)
+        plane2 = keep.tile([P, S], U8, name="plane2", align_bytes=64)
+        planes = (gb, plane1, plane2)
+        w_t = keep.tile([P, E * PASSES * 2 * N], U8, name="w_t", align_bytes=64)
+        ws_t = keep.tile([P, E * PASSES, N], U8, name="ws_t", align_bytes=64)
+        b_t = keep.tile([P, E], F32, name="b_t")
+        gate_t = [keep.tile([P, T], F32, name=f"gate_t{i}", align_bytes=64) for i in range(2)]
+        y = keep.tile([P, S], F32, name="y", align_bytes=64)
+        warm = keep.tile([P, 2], F32, name="warm")
+
+        raw = {}
+        for a in range(PASSES):
+            rows = xT[a * 512 : (a + 1) * 512, :].rearrange("(p j) t -> p j t", j=PACK)
+            for c, (c0, n) in enumerate(chunks[a]):
+                r = keep.tile([P, PACK, n], F32, name=f"raw{a}_{c}", align_bytes=64)
+                nc.sync.dma_start(out=r[:], in_=rows[:, :, c0 : c0 + n])
+                raw[a, c] = r
+                if (a, c) == (0, 0):
+                    nc.sync.dma_start(offs_t[:], offs)
+
+        nc.gpsimd.memset(bytes_all[:].bitcast(I32), 0)
+        nc.gpsimd.memset(ws_t[:].rearrange("p a n -> p (a n)").bitcast(I32), 0)
+        nc.gpsimd.memset(plane1[:].bitcast(I32), 0)
+        nc.gpsimd.memset(plane2[:].bitcast(I32), 0)
+        nc.gpsimd.memset(warm[:], 0.0)
+        nc.scalar.activation(warm[:, 1:2], warm[:, 0:1], GELU)
+
+        ws_i = ws_t[:].bitcast(I32)
+        ws_d = w_scales.bitcast(I32).rearrange("e a q n -> q (e a) n")
+        for quad in range(4):
+            nc.sync.dma_start(out=ws_i[32 * quad : 32 * quad + 4], in_=ws_d[4 * quad : 4 * quad + 4])
+        nc.sync.dma_start(
+            out=w_t[:].bitcast(I32).rearrange("p (i n) -> p i n", n=N // 2),
+            in_=w_words.bitcast(I32).rearrange("e a p n -> p (e a) n"),
+        )
+        nc.sync.dma_start(out=b_t[:], in_=b)
+        for i in range(2):
+            nc.sync.dma_start(out=gate_t[i][:], in_=gate[i])
+        nc.sync.dma_start(pos1_t[:], pos1)
+        nc.sync.dma_start(pos2_t[:], pos2)
+
+        def quantise(a):
+            for c, (c0, n) in enumerate(chunks[a]):
+                g = keep.tile([P, n, PACK], BF16, name=f"g{a}_{c}", align_bytes=64)
+                src = raw[a, c][:].rearrange("p j w -> p w j")
+                if (a, c) in vector_copies:
+                    nc.vector.tensor_copy(out=g[:], in_=src)
+                else:
+                    nc.scalar.copy(out=g[:], in_=src)
+                nc.vector.quantize_mx(
+                    out=codes[a][:, c0 : c0 + n].bitcast(FP8X4),
+                    scales=bytes_all[4 * a : P, c0 : c0 + n],
+                    in_=g[:].rearrange("p w j -> p (w j)"),
+                )
+
+        def gather_words(a, s0, s1):
+            nc.vector.tensor_copy(
+                out=gw[a][:, s0:s1], in_=codes[a][:].indirect(offs_t[:, s0 // 16 : s1 // 16])
+            )
+
+        thirds = ((0, 1024), (1024, 2048), (2048, 3072))
+        for a in (0, 1):
+            quantise(a)
+            for s0, s1 in thirds:
+                gather_words(a, s0, s1)
+        quantise(2)
+
+        banks = [psum.tile([P, 512], F32, name=f"bank{i}") for i in range(8)]
+
+        def multiply(e, s0, n, dst, passes):
+            for a in passes:
+                i = PASSES * e + a
+                nc.tensor.matmul_mx(
+                    out=dst,
+                    lhsT=w_t[:, 2 * N * i : 2 * N * (i + 1)].bitcast(FP4X4),
+                    lhsT_scale=ws_t[:, i, :],
+                    rhs=gw[a][:, s0 : s0 + n].bitcast(FP8X4),
+                    rhs_scale=planes[a][:, s0 : s0 + n],
+                    start=(a == 0),
+                    stop=(a == PASSES - 1),
+                )
+
+        def activate(e, s0, n, src):
+            nc.scalar.activation(y[:, s0 : s0 + n], src, GELU, bias=b_t[:, e : e + 1])
+
+        e2 = (2, 256, 512, banks[0][:])
+        e4a = (4, 896, 512, banks[1][:])
+        e6a = (6, 1920, 512, banks[2][:])
+        e7 = (7, 2560, 512, banks[3][:])
+        e0 = (0, 0, 128, banks[4][:, 0:128])
+        e1 = (1, 128, 128, banks[5][:, 0:128])
+        e3 = (3, 768, 128, banks[6][:, 0:128])
+        e4b = (4, 1408, 128, banks[6][:, 128:256])
+        e6b = (6, 2432, 128, banks[6][:, 256:384])
+        e5 = [(5, 1536 + 128 * i, 128, banks[7][:, 128 * i : 128 * (i + 1)]) for i in range(3)]
+
+        def gather_bytes(s0, s1):
+            nc.vector.tensor_copy(
+                out=gb[:, s0:s1], in_=bytes_all[:].indirect(offs_t[:, s0 // 16 : s1 // 16])
+            )
+            for a in (1, 2):
+                nc.scalar.dma_start(
+                    out=planes[a][0:112, s0:s1].bitcast(I32),
+                    in_=gb[4 * a : 4 * a + 112, s0:s1].bitcast(I32),
+                )
+
+        def partial(a, *groups):
+            for group in groups:
+                multiply(*group, (a,))
+
+        gather_bytes(0, 896)
+        partial(0, e2, e0, e1)
+        gather_bytes(896, 1920)
+        partial(0, e4a)
+        partial(1, e2, e0, e1)
+        gather_bytes(1920, 3072)
+        partial(0, e6a, e7)
+        partial(1, e4a)
+        gather_words(2, 256, 896)
+        partial(2, e2)
+        activate(*e2)
+        multiply(*e3, range(3))
+        activate(*e3)
+        gather_words(2, 896, 1536)
+        partial(2, e4a)
+        activate(*e4a)
+        multiply(*e4b, range(3))
+        activate(*e4b)
+        partial(1, e6a, e7)
+        gather_words(2, 1536, 2560)
+        for group in e5:
+            multiply(*group, range(3))
+        activate(5, 1536, 384, banks[7][:, 0:384])
+        partial(2, e6a)
+        activate(*e6a)
+        multiply(*e6b, range(3))
+        activate(*e6b)
+        gather_words(2, 2560, 3072)
+        partial(2, e7)
+        activate(*e7)
+        gather_words(2, 0, 256)
+        for group in (e0, e1):
+            partial(2, group)
+            activate(*group)
+
+        parts = ((0, 512), (512, 512), (1024, 256), (1280, 256))
+        first = [keep.tile([P, n], F32, name=f"first{i}") for i, (t0, n) in enumerate(parts)]
+        second = [keep.tile([P, n], F32, name=f"second{i}") for i, (t0, n) in enumerate(parts)]
+        total = [keep.tile([P, n], F32, name=f"total{i}") for i, (t0, n) in enumerate(parts)]
+
+        def pick(i, dst, which, pos_t):
+            t0, n = parts[i]
+            nc.vector.tensor_tensor(
+                dst[i][:],
+                y[:].indirect(pos_t[:, t0 // 16 : (t0 + n) // 16]),
+                gate_t[which][:, t0 : t0 + n],
+                MULT,
+            )
+
+        def add_and_store(i):
+            t0, n = parts[i]
+            nc.vector.tensor_add(out=total[i][:], in0=first[i][:], in1=second[i][:])
+            nc.sync.dma_start(out=out[:, t0 : t0 + n], in_=total[i][:])
+
+        for i in range(len(parts)):
+            pick(i, first, 0, pos1_t)
+            if i > 0:
+                add_and_store(i - 1)
+            pick(i, second, 1, pos2_t)
+        add_and_store(len(parts) - 1)

@@ -36,12 +36,12 @@ def tile_moe_rag_lin_gelu_kernel(tc, xT, w_words, w_scales, b, gate, offs, pos1,
         pos1_t = lists.tile([P, T // 16], U16, name="pos1_t")
         pos2_t = lists.tile([P, T // 16], U16, name="pos2_t")
 
-        chunks = (
-            ((0, 512), (512, 512), (1024, 256), (1280, 256)),
-            ((0, 512), (512, 512), (1024, 256), (1280, 256)),
-            ((0, 512), (512, 512), (1024, 512)),
+        pieces = (
+            ((0, 512, "v"), (512, 512, "s"), (1024, 256, "v"), (1280, 128, "v"), (1408, 128, "s")),
+            ((0, 512, "s"), (512, 512, "s"), (1024, 512, "s")),
+            ((0, 512, "s"), (512, 512, "s"), (1024, 512, "s")),
         )
-        vector_copies = {(0, 0), (0, 2), (0, 3)}
+        loads = ((512, 512, 256, 256), (512, 512, 512), (512, 512, 512))
 
         codes = [keep.tile([P, T], U32, name=f"codes{a}", align_bytes=64) for a in range(PASSES)]
         bytes_all = keep.tile([P, T], U8, name="bytes_all", align_bytes=64)
@@ -60,11 +60,13 @@ def tile_moe_rag_lin_gelu_kernel(tc, xT, w_words, w_scales, b, gate, offs, pos1,
         raw = {}
         for a in range(PASSES):
             rows = xT[a * 512 : (a + 1) * 512, :].rearrange("(p j) t -> p j t", j=PACK)
-            for c, (c0, n) in enumerate(chunks[a]):
-                r = keep.tile([P, PACK, n], F32, name=f"raw{a}_{c}", align_bytes=64)
+            c0 = 0
+            for n in loads[a]:
+                r = keep.tile([P, PACK, n], F32, name=f"raw{a}_{c0}", align_bytes=64)
                 nc.sync.dma_start(out=r[:], in_=rows[:, :, c0 : c0 + n])
-                raw[a, c] = r
-                if (a, c) == (0, 0):
+                raw[a, c0] = r
+                c0 += n
+                if len(raw) == 1:
                     nc.sync.dma_start(offs_t[:], offs)
 
         nc.gpsimd.memset(bytes_all[:].bitcast(I32), 0)
@@ -89,13 +91,15 @@ def tile_moe_rag_lin_gelu_kernel(tc, xT, w_words, w_scales, b, gate, offs, pos1,
         nc.sync.dma_start(pos2_t[:], pos2)
 
         def quantise(a):
-            for c, (c0, n) in enumerate(chunks[a]):
-                g = keep.tile([P, n, PACK], BF16, name=f"g{a}_{c}", align_bytes=64)
-                src = raw[a, c][:].rearrange("p j w -> p w j")
-                if (a, c) in vector_copies:
-                    nc.vector.tensor_copy(out=g[:], in_=src)
+            for c0, n, engine in pieces[a]:
+                g = keep.tile([P, n, PACK], BF16, name=f"g{a}_{c0}", align_bytes=64)
+                start = max(s for p, s in raw if p == a and s <= c0)
+                src = raw[a, start][:, :, c0 - start : c0 - start + n].rearrange("p j (c i) -> p c j i", i=4)
+                dst = g[:].rearrange("p (c i) j -> p c j i", i=4)
+                if engine == "v":
+                    nc.vector.tensor_copy(out=dst, in_=src)
                 else:
-                    nc.scalar.copy(out=g[:], in_=src)
+                    nc.scalar.copy(out=dst, in_=src)
                 nc.vector.quantize_mx(
                     out=codes[a][:, c0 : c0 + n].bitcast(FP8X4),
                     scales=bytes_all[4 * a : P, c0 : c0 + n],
@@ -192,7 +196,7 @@ def tile_moe_rag_lin_gelu_kernel(tc, xT, w_words, w_scales, b, gate, offs, pos1,
             partial(2, group)
             activate(*group)
 
-        parts = ((0, 512), (512, 512), (1024, 256), (1280, 256))
+        parts = ((0, 512), (512, 512), (1024, 352), (1376, 160))
         first = [keep.tile([P, n], F32, name=f"first{i}") for i, (t0, n) in enumerate(parts)]
         second = [keep.tile([P, n], F32, name=f"second{i}") for i, (t0, n) in enumerate(parts)]
         total = [keep.tile([P, n], F32, name=f"total{i}") for i, (t0, n) in enumerate(parts)]
@@ -213,7 +217,8 @@ def tile_moe_rag_lin_gelu_kernel(tc, xT, w_words, w_scales, b, gate, offs, pos1,
 
         for i in range(len(parts)):
             pick(i, first, 0, pos1_t)
-            if i > 0:
+            if 0 < i < len(parts) - 1:
                 add_and_store(i - 1)
             pick(i, second, 1, pos2_t)
+        add_and_store(len(parts) - 2)
         add_and_store(len(parts) - 1)

@@ -38,9 +38,10 @@ def tile_moe_rag_lin_gelu_kernel(tc, xT, w_words, w_scales, b, gate, offs, pos1,
 
         pieces = (
             ((0, 512, "v"), (512, 512, "s"), (1024, 256, "v"), (1280, 128, "v"), (1408, 128, "s")),
-            ((0, 512, "s"), (512, 512, "s"), (1024, 512, "s")),
+            ((0, 512, "s"), (512, 512, "s"), (1024, 512, "b")),
             ((0, 512, "s"), (512, 512, "s"), (1024, 512, "s")),
         )
+        shared = 384
         loads = ((512, 512, 256, 256), (512, 512, 512), (512, 512, 512))
 
         codes = [keep.tile([P, T], U32, name=f"codes{a}", align_bytes=64) for a in range(PASSES)]
@@ -66,8 +67,8 @@ def tile_moe_rag_lin_gelu_kernel(tc, xT, w_words, w_scales, b, gate, offs, pos1,
                 nc.sync.dma_start(out=r[:], in_=rows[:, :, c0 : c0 + n])
                 raw[a, c0] = r
                 c0 += n
-                if len(raw) == 1:
-                    nc.sync.dma_start(offs_t[:], offs)
+            if a == 0:
+                nc.sync.dma_start(offs_t[:], offs)
 
         nc.gpsimd.memset(bytes_all[:].bitcast(I32), 0)
         nc.gpsimd.memset(ws_t[:].rearrange("p a n -> p (a n)").bitcast(I32), 0)
@@ -96,10 +97,11 @@ def tile_moe_rag_lin_gelu_kernel(tc, xT, w_words, w_scales, b, gate, offs, pos1,
                 start = max(s for p, s in raw if p == a and s <= c0)
                 src = raw[a, start][:, :, c0 - start : c0 - start + n].rearrange("p j (c i) -> p c j i", i=4)
                 dst = g[:].rearrange("p (c i) j -> p c j i", i=4)
-                if engine == "v":
-                    nc.vector.tensor_copy(out=dst, in_=src)
-                else:
-                    nc.scalar.copy(out=dst, in_=src)
+                mid = {"v": 0, "s": n, "b": shared}[engine] // 4
+                if mid > 0:
+                    nc.scalar.copy(out=dst[:, :mid], in_=src[:, :mid])
+                if mid < n // 4:
+                    nc.vector.tensor_copy(out=dst[:, mid:], in_=src[:, mid:])
                 nc.vector.quantize_mx(
                     out=codes[a][:, c0 : c0 + n].bitcast(FP8X4),
                     scales=bytes_all[4 * a : P, c0 : c0 + n],
@@ -196,7 +198,7 @@ def tile_moe_rag_lin_gelu_kernel(tc, xT, w_words, w_scales, b, gate, offs, pos1,
             partial(2, group)
             activate(*group)
 
-        parts = ((0, 512), (512, 512), (1024, 352), (1376, 160))
+        parts = ((0, 832), (832, 512), (1344, 192))
         first = [keep.tile([P, n], F32, name=f"first{i}") for i, (t0, n) in enumerate(parts)]
         second = [keep.tile([P, n], F32, name=f"second{i}") for i, (t0, n) in enumerate(parts)]
         total = [keep.tile([P, n], F32, name=f"total{i}") for i, (t0, n) in enumerate(parts)]
@@ -217,8 +219,7 @@ def tile_moe_rag_lin_gelu_kernel(tc, xT, w_words, w_scales, b, gate, offs, pos1,
 
         for i in range(len(parts)):
             pick(i, first, 0, pos1_t)
-            if 0 < i < len(parts) - 1:
+            if i > 0:
                 add_and_store(i - 1)
             pick(i, second, 1, pos2_t)
-        add_and_store(len(parts) - 2)
         add_and_store(len(parts) - 1)

from contextlib import ExitStack

import concourse.mybir as mybir

F32 = mybir.dt.float32
BF16 = mybir.dt.bfloat16
I32 = mybir.dt.int32
U32 = mybir.dt.uint32
U16 = mybir.dt.uint16
U8 = mybir.dt.uint8
FP8X4 = mybir.dt.float8_e4m3fn_x4
FP4X4 = mybir.dt.float4_e2m1fn_x4
GELU = mybir.ActivationFunctionType.Gelu_apprx_tanh
MULT = mybir.AluOpType.mult

P = 128
PACK = 4
K = 1536
T = 1536
PASSES = 3
E = 8
N = 128
S = 3072
COUNTS = (128, 128, 512, 128, 640, 384, 640, 512)
FLOPS = 2 * S * K * N


def tile_moe_rag_lin_gelu_kernel(tc, xT, w_words, w_scales, b, gate, offs, pos1, pos2, out):
    nc = tc.nc
    with ExitStack() as ctx:
        lists = ctx.enter_context(tc.tile_pool(name="lists", bufs=1))
        keep = ctx.enter_context(tc.tile_pool(name="keep", bufs=1))
        psum = ctx.enter_context(tc.psum_pool(name="psum", bufs=1))

        offs_t = lists.tile([P, S // 16], U16, name="offs_t")
        pos1_t = lists.tile([P, T // 16], U16, name="pos1_t")
        pos2_t = lists.tile([P, T // 16], U16, name="pos2_t")

        pieces = (
            ((0, 512, "v"), (512, 512, "s"), (1024, 256, "v"), (1280, 128, "v"), (1408, 128, "s")),
            ((0, 512, "s"), (512, 512, "s"), (1024, 512, "b")),
            ((0, 512, "s"), (512, 512, "s"), (1024, 512, "s")),
        )
        shared = 384
        loads = ((512, 512, 256, 256), (512, 512, 512), (512, 512, 512))

        codes = [keep.tile([P, T], U32, name=f"codes{a}", align_bytes=64) for a in range(PASSES)]
        bytes_all = keep.tile([P, T], U8, name="bytes_all", align_bytes=64)
        gw = [keep.tile([P, S], U32, name=f"gw{a}", align_bytes=64) for a in range(PASSES)]
        gb = keep.tile([P, S], U8, name="gb", align_bytes=64)
        plane1 = keep.tile([P, S], U8, name="plane1", align_bytes=64)
        plane2 = keep.tile([P, S], U8, name="plane2", align_bytes=64)
        planes = (gb, plane1, plane2)
        w_t = keep.tile([P, E * PASSES * 2 * N], U8, name="w_t", align_bytes=64)
        ws_t = keep.tile([P, E * PASSES, N], U8, name="ws_t", align_bytes=64)
        b_t = keep.tile([P, E], F32, name="b_t")
        gate_t = [keep.tile([P, T], F32, name=f"gate_t{i}", align_bytes=64) for i in range(2)]
        y = keep.tile([P, S], F32, name="y", align_bytes=64)
        warm = keep.tile([P, 2], F32, name="warm")

        raw = {}
        for a in range(PASSES):
            rows = xT[a * 512 : (a + 1) * 512, :].rearrange("(p j) t -> p j t", j=PACK)
            c0 = 0
            for n in loads[a]:
                r = keep.tile([P, PACK, n], F32, name=f"raw{a}_{c0}", align_bytes=64)
                nc.sync.dma_start(out=r[:], in_=rows[:, :, c0 : c0 + n])
                raw[a, c0] = r
                c0 += n
            if a == 0:
                nc.sync.dma_start(offs_t[:], offs)

        nc.gpsimd.memset(bytes_all[:].bitcast(I32), 0)
        nc.gpsimd.memset(ws_t[:].rearrange("p a n -> p (a n)").bitcast(I32), 0)
        nc.gpsimd.memset(plane1[:].bitcast(I32), 0)
        nc.gpsimd.memset(plane2[:].bitcast(I32), 0)
        nc.gpsimd.memset(warm[:], 0.0)
        nc.scalar.activation(warm[:, 1:2], warm[:, 0:1], GELU)

        ws_i = ws_t[:].bitcast(I32)
        ws_d = w_scales.bitcast(I32).rearrange("e a q n -> q (e a) n")
        for quad in range(4):
            nc.sync.dma_start(out=ws_i[32 * quad : 32 * quad + 4], in_=ws_d[4 * quad : 4 * quad + 4])
        nc.sync.dma_start(
            out=w_t[:].bitcast(I32).rearrange("p (i n) -> p i n", n=N // 2),
            in_=w_words.bitcast(I32).rearrange("e a p n -> p (e a) n"),
        )
        nc.sync.dma_start(out=b_t[:], in_=b)
        for i in range(2):
            nc.sync.dma_start(out=gate_t[i][:], in_=gate[i])
        nc.sync.dma_start(pos1_t[:], pos1)
        nc.sync.dma_start(pos2_t[:], pos2)

        def quantise(a):
            for c0, n, engine in pieces[a]:
                g = keep.tile([P, n, PACK], BF16, name=f"g{a}_{c0}", align_bytes=64)
                start = max(s for p, s in raw if p == a and s <= c0)
                src = raw[a, start][:, :, c0 - start : c0 - start + n].rearrange("p j (c i) -> p c j i", i=4)
                dst = g[:].rearrange("p (c i) j -> p c j i", i=4)
                mid = {"v": 0, "s": n, "b": shared}[engine] // 4
                if mid > 0:
                    nc.scalar.copy(out=dst[:, :mid], in_=src[:, :mid])
                if mid < n // 4:
                    nc.vector.tensor_copy(out=dst[:, mid:], in_=src[:, mid:])
                nc.vector.quantize_mx(
                    out=codes[a][:, c0 : c0 + n].bitcast(FP8X4),
                    scales=bytes_all[4 * a : P, c0 : c0 + n],
                    in_=g[:].rearrange("p w j -> p (w j)"),
                )

        def gather_words(a, s0, s1):
            nc.vector.tensor_copy(
                out=gw[a][:, s0:s1], in_=codes[a][:].indirect(offs_t[:, s0 // 16 : s1 // 16])
            )

        thirds = ((0, 1024), (1024, 2048), (2048, 3072))
        for a in (0, 1):
            quantise(a)
            for s0, s1 in thirds:
                gather_words(a, s0, s1)
        quantise(2)

        banks = [psum.tile([P, 512], F32, name=f"bank{i}") for i in range(8)]

        def multiply(e, s0, n, dst, passes):
            for a in passes:
                i = PASSES * e + a
                nc.tensor.matmul_mx(
                    out=dst,
                    lhsT=w_t[:, 2 * N * i : 2 * N * (i + 1)].bitcast(FP4X4),
                    lhsT_scale=ws_t[:, i, :],
                    rhs=gw[a][:, s0 : s0 + n].bitcast(FP8X4),
                    rhs_scale=planes[a][:, s0 : s0 + n],
                    start=(a == 0),
                    stop=(a == PASSES - 1),
                )

        def activate(e, s0, n, src):
            nc.scalar.activation(y[:, s0 : s0 + n], src, GELU, bias=b_t[:, e : e + 1])

        e2 = (2, 256, 512, banks[0][:])
        e4a = (4, 896, 512, banks[1][:])
        e6a = (6, 1920, 512, banks[2][:])
        e7 = (7, 2560, 512, banks[3][:])
        e0 = (0, 0, 128, banks[4][:, 0:128])
        e1 = (1, 128, 128, banks[5][:, 0:128])
        e3 = (3, 768, 128, banks[6][:, 0:128])
        e4b = (4, 1408, 128, banks[6][:, 128:256])
        e6b = (6, 2432, 128, banks[6][:, 256:384])
        e5 = [(5, 1536 + 128 * i, 128, banks[7][:, 128 * i : 128 * (i + 1)]) for i in range(3)]

        def gather_bytes(s0, s1):
            nc.vector.tensor_copy(
                out=gb[:, s0:s1], in_=bytes_all[:].indirect(offs_t[:, s0 // 16 : s1 // 16])
            )
            for a in (1, 2):
                nc.scalar.dma_start(
                    out=planes[a][0:112, s0:s1].bitcast(I32),
                    in_=gb[4 * a : 4 * a + 112, s0:s1].bitcast(I32),
                )

        def partial(a, *groups):
            for group in groups:
                multiply(*group, (a,))

        gather_bytes(0, 896)
        partial(0, e2, e0, e1)
        gather_bytes(896, 1920)
        partial(0, e4a)
        partial(1, e2, e0, e1)
        gather_bytes(1920, 3072)
        partial(0, e6a, e7)
        partial(1, e4a)
        gather_words(2, 256, 896)
        partial(2, e2)
        activate(*e2)
        multiply(*e3, range(3))
        activate(*e3)
        gather_words(2, 896, 1536)
        partial(2, e4a)
        activate(*e4a)
        multiply(*e4b, range(3))
        activate(*e4b)
        partial(1, e6a, e7)
        gather_words(2, 1536, 2560)
        for group in e5:
            multiply(*group, range(3))
        activate(5, 1536, 384, banks[7][:, 0:384])
        partial(2, e6a)
        activate(*e6a)
        multiply(*e6b, range(3))
        activate(*e6b)
        gather_words(2, 2560, 3072)
        partial(2, e7)
        activate(*e7)
        gather_words(2, 0, 256)
        for group in (e0, e1):
            partial(2, group)
            activate(*group)

        parts = ((0, 832), (832, 512), (1344, 192))
        first = [keep.tile([P, n], F32, name=f"first{i}") for i, (t0, n) in enumerate(parts)]
        second = [keep.tile([P, n], F32, name=f"second{i}") for i, (t0, n) in enumerate(parts)]
        total = [keep.tile([P, n], F32, name=f"total{i}") for i, (t0, n) in enumerate(parts)]

        def pick(i, dst, which, pos_t):
            t0, n = parts[i]
            nc.vector.tensor_tensor(
                dst[i][:],
                y[:].indirect(pos_t[:, t0 // 16 : (t0 + n) // 16]),
                gate_t[which][:, t0 : t0 + n],
                MULT,
            )

        def add_and_store(i):
            t0, n = parts[i]
            nc.vector.tensor_add(out=total[i][:], in0=first[i][:], in1=second[i][:])
            nc.sync.dma_start(out=out[:, t0 : t0 + n], in_=total[i][:])

        for i in range(len(parts)):
            pick(i, first, 0, pos1_t)
            if i > 0:
                add_and_store(i - 1)
            pick(i, second, 1, pos2_t)
        add_and_store(len(parts) - 1)
